import numpy as np
import ml_dtypes


def mxq(x, axis, fmt="e4m3"):
    dtype, down = {"e4m3": (ml_dtypes.float8_e4m3fn, 7), "e5m2": (ml_dtypes.float8_e5m2, 14)}[fmt]
    v = np.moveaxis(np.asarray(x, np.float32).astype(ml_dtypes.bfloat16).astype(np.float64), axis, -1)
    blocks = v.reshape(v.shape[:-1] + (-1, 32))
    amax = np.abs(blocks).max(-1, keepdims=True)
    byte = np.maximum(np.where(amax > 0, np.frexp(amax)[1] - 1 + 127, 0) - down, 1)
    scale = np.exp2(byte - 127.0)
    codes = (blocks / scale).astype(np.float32).astype(dtype).astype(np.float64)
    return np.moveaxis((codes * scale).reshape(v.shape), -1, axis)


WIDE = False


def mx_kscale(k):
    if not WIDE:
        return np.ones(k)
    levels = np.array([10, -10, 5, -5, 0])
    if k % 512:
        return np.exp2(np.random.permutation(np.resize(levels, k // 32))).repeat(32)
    a = np.empty((k // 512, 16))
    for p in range(k // 512):
        a[p, :8] = np.random.permutation(np.resize(levels, 8))
        for g in range(8):
            far = levels[np.abs(levels - a[p, g]) >= 10]
            a[p, g + 8] = far[np.random.randint(len(far))]
    return np.exp2(a.ravel()).repeat(32)


def f64(x):
    return np.asarray(x).astype(np.float64)


E2M1 = np.array([0.0, 0.5, 1.0, 1.5, 2.0, 3.0, 4.0, 6.0, -0.0, -0.5, -1.0, -1.5, -2.0, -3.0, -4.0, -6.0])


def pack_weight(w, fmt):
    k, n = w.shape
    w = f64(np.asarray(w, np.float32).astype(ml_dtypes.bfloat16)).reshape(k // 32, 32, n)
    amax = np.abs(w).max(1)
    if fmt == "e4m3":
        byte = np.frexp(amax)[1] - 1 + 127 - 7
    else:
        mant, ex = np.frexp(amax / 6.0)
        byte = np.where(mant > 0.5, ex, ex - 1) + 127
    byte = np.clip(np.where(amax > 0, byte, 1), 1, 254)
    scaled = (w * np.exp2(127.0 - byte)[:, None, :]).reshape(k, n).astype(np.float32)
    by_word = np.ascontiguousarray(scaled.reshape(k // 512, 128, 4, n).transpose(0, 1, 3, 2))
    if fmt == "e4m3":
        words = by_word.astype(ml_dtypes.float8_e4m3fn).view(np.uint8)
    else:
        c = by_word.astype(ml_dtypes.float4_e2m1fn).view(np.uint8) & 0xF
        words = (c[..., 0::2] | (c[..., 1::2] << 4)).reshape(k // 512, 128, 2 * n)
    return np.ascontiguousarray(words), np.ascontiguousarray(byte.astype(np.uint8).reshape(k // 512, 16, n))


def unpack_weight(words, scales, fmt):
    g, _, n = scales.shape
    words = np.ascontiguousarray(words).reshape(g, 128, n, -1)
    if fmt == "e4m3":
        vals = words.view(ml_dtypes.float8_e4m3fn).astype(np.float64)
    else:
        nib = np.empty((g, 128, n, 4), np.uint8)
        nib[..., 0::2] = words & 0xF
        nib[..., 1::2] = words >> 4
        vals = E2M1[nib]
    vals = vals * np.repeat(np.exp2(scales.astype(np.float64) - 127.0), 8, axis=1)[..., None]
    return vals.transpose(0, 1, 3, 2).reshape(g * 512, n)


def planes(y):
    n, m = y.shape
    v = y.astype(np.float32).astype(ml_dtypes.bfloat16).astype(np.float64).reshape(n // 32, 32, m)
    top = np.abs(v).max(1)
    byte = np.clip(np.where(top > 0, np.frexp(top)[1] - 1 + 127 - 7, 1), 1, 254)
    codes = (v * np.exp2(127.0 - byte)[:, None, :]).reshape(n, m).astype(np.float32).astype(ml_dtypes.float8_e4m3fn).view(np.uint8)
    words = codes.reshape(n // 512, 128, 4, m).transpose(0, 1, 3, 2)
    return np.ascontiguousarray(words), np.ascontiguousarray(byte.astype(np.uint8).reshape(n // 512, 16, m))


D, K, M, T = 64, 1024, 1024, 512


def setup_inputs():
    n = np.random.standard_normal
    s = mx_kscale(K)[:, None]
    p_w0 = pack_weight(n((K, M)) / np.sqrt(K) / s, "e2m1")
    p_w1 = pack_weight(n((K, M)) / np.sqrt(K) / s, "e4m3")
    return {
        "x": (n((K, T + 2 * D)) * s).astype(np.float32),
        "w0_words": p_w0[0],
        "w0_scales": p_w0[1],
        "w1_words": p_w1[0],
        "w1_scales": p_w1[1],
        "w2": (n((K, M)) / np.sqrt(K) / s).astype(np.float32),
    }


def reference(x, w0_words, w0_scales, w1_words, w1_scales, w2):
    x_ = mxq(f64(x), 0, "e4m3")
    w0_ = unpack_weight(w0_words, w0_scales, "e2m1")
    w1_ = unpack_weight(w1_words, w1_scales, "e4m3")
    w2_ = mxq(f64(w2), 0, "e4m3")
    y = w0_.T @ x_[:, :T] + w1_.T @ x_[:, D:D + T] + w2_.T @ x_[:, 2 * D:]
    out_0 = y
    return (out_0,) + planes(out_0)

@@ -1,0 +1,282 @@
+from contextlib import ExitStack
+
+import concourse.mybir as mybir
+
+D, K, M, T = 64, 1024, 1024, 512
+FLOPS = 2 * 3 * K * M * T
+
+F32 = mybir.dt.float32
+BF16 = mybir.dt.bfloat16
+I32 = mybir.dt.int32
+U32 = mybir.dt.uint32
+U8 = mybir.dt.uint8
+FP8X4 = mybir.dt.float8_e4m3fn_x4
+FP4X4 = mybir.dt.float4_e2m1fn_x4
+
+P = 128
+PACK = 4
+G = P * PACK
+XW = T + 2 * D
+W1_ROW = 4
+
+
+def tile_mix_dconv_fm_pl_none_kernel(
+    tc, x, w0_words, w0_scales, w1_words, w1_scales, w2, out_0, out_1, out_2
+):
+    nc = tc.nc
+    with ExitStack() as ctx:
+        sb = ctx.enter_context(tc.tile_pool(name="sb", bufs=1))
+        ps = ctx.enter_context(tc.psum_pool(name="ps", bufs=1))
+        ctx.enter_context(tc.manual_schedule())
+
+        def tile(name, width, dtype):
+            return sb.tile([P, width], dtype, name=name, align_bytes=64)
+
+        AH = [(a, h) for a in range(2) for h in range(2)]
+        x_raw = {}
+        x_bf = [tile("x_bf%d" % a, PACK * XW, BF16) for a in range(2)]
+        x_codes = [tile("x_codes%d" % a, XW, U32) for a in range(2)]
+        x_scales = [tile("x_scales%d" % a, XW, U8) for a in range(2)]
+        w0_raw = [tile("w0_raw%d" % a, 2 * M, U8) for a in range(2)]
+        w0_codes = {ah: tile("w0_codes%d%d" % ah, 2 * G, U8) for ah in AH}
+        w1_raw = {}
+        w1_codes = {ah: tile("w1_codes%d%d" % ah, G, U32) for ah in AH}
+        s0_raw = tile("s0_raw", 2 * M, U8)
+        s1_raw = tile("s1_raw", 2 * M, U8)
+        s0 = [tile("s0_%d" % a, M, U8) for a in range(2)]
+        s1 = [tile("s1_%d" % a, M, U8) for a in range(2)]
+        w2_bf = {ah: tile("w2_bf%d%d" % ah, PACK * G, BF16) for ah in AH}
+        w2_codes = {ah: tile("w2_codes%d%d" % ah, G, U32) for ah in AH}
+        w2_scales = {ah: tile("w2_scales%d%d" % ah, G, U8) for ah in AH}
+        y = [tile("y%d" % h, PACK * T, F32) for h in range(2)]
+        y_bf = [tile("y_bf%d" % h, PACK * T, BF16) for h in range(2)]
+        y_codes = [tile("y_codes%d" % h, T, U32) for h in range(2)]
+        y_scales = tile("y_scales", 2 * T, U8)
+        acc = {(h, r): ps.tile([P, T], F32, name="acc%d%d" % (h, r)) for h in range(2) for r in range(PACK)}
+        w2_raw = {}
+
+        def copy(engine, out, in_):
+            if engine == "V":
+                nc.vector.tensor_copy(out=out, in_=in_)
+            else:
+                nc.scalar.copy(out=out, in_=in_)
+
+        def load_x(a, c0, c1):
+            raw = tile("x_raw%d_%d" % (a, c0), PACK * (c1 - c0), F32)
+            x_raw[a, c0] = raw
+            nc.sync.dma_start(
+                out=raw[:].rearrange("p (j t) -> p j t", j=PACK),
+                in_=x[a * G : (a + 1) * G, c0:c1].rearrange("(p j) t -> p j t", j=PACK),
+            )
+
+        def load_w0(a):
+            nc.sync.dma_start(out=w0_raw[a][:].bitcast(I32), in_=w0_words[a].bitcast(I32))
+
+        def load_w1(a0, a1, h0, h1):
+            width = G * (h1 - h0)
+            raw = tile("w1_raw%d%d" % (a0, h0), width * (a1 - a0), U32)
+            for a in range(a0, a1):
+                for h in range(h0, h1):
+                    c0 = width * (a - a0) + G * (h - h0)
+                    w1_raw[a, h] = raw[:, c0 : c0 + G]
+            src = w1_words.rearrange("a p n i -> p a (n i)")[:, a0:a1, PACK * G * h0 : PACK * G * h1]
+            nc.sync.dma_start(
+                out=raw[:].bitcast(I32).rearrange("p (a n) -> p a n", a=a1 - a0), in_=src.bitcast(I32)
+            )
+
+        def load_scales(raw, src, row):
+            for r in range(4):
+                nc.sync.dma_start(
+                    out=raw[row + r : P : 32, :].bitcast(I32).rearrange("q (a w) -> q a w", a=2),
+                    in_=src.rearrange("a (q r) n -> r q a n", r=4)[r].bitcast(I32),
+                )
+
+        def load_w2(a, h, m0, m1):
+            width = PACK * (m1 - m0)
+            raw = tile("w2_raw%d%d_%d" % (a, h, m0), PACK * width, F32)
+            w2_raw[a, h, m0] = raw
+            n0 = G * h + PACK * m0
+            nc.sync.dma_start(
+                out=raw[:].rearrange("p (j n) -> p j n", j=PACK),
+                in_=w2[a * G : (a + 1) * G, n0 : n0 + width].rearrange("(p j) n -> p j n", j=PACK),
+            )
+
+        def interleave(engine, dst, src, c0, c1, first=0):
+            out = dst[:, PACK * c0 : PACK * c1].rearrange("p (c i j) -> p c j i", i=4, j=PACK)
+            in_ = src[:].rearrange("p (j t) -> p j t", j=PACK)[:, :, c0 - first : c1 - first].rearrange("p j (c i) -> p c j i", i=4)
+            copy(engine, out, in_)
+
+        def quantize(codes, scales, src, c0, c1, s_off=0):
+            nc.vector.quantize_mx(
+                out=codes[:, c0:c1].bitcast(FP8X4),
+                scales=scales[:, s_off + c0 : s_off + c1],
+                in_=src[:, PACK * c0 : PACK * c1],
+            )
+
+        def round_w2(engine, a, h, piece, m0, m1):
+            out = w2_bf[a, h][:].rearrange("p (r m j) -> p m j r", r=PACK, j=PACK)[:, m0:m1]
+            in_ = w2_raw[a, h, piece][:].rearrange("p (j m r) -> p m j r", r=PACK, j=PACK)[:, m0 - piece : m1 - piece]
+            copy(engine, out, in_)
+
+        def quantize_w2(a, h, c0, c1):
+            quantize(w2_codes[a, h], w2_scales[a, h], w2_bf[a, h], c0, c1)
+
+        def deal_w0(a, h):
+            nc.vector.tensor_copy(
+                out=w0_codes[a, h][:].rearrange("p (r m b) -> p r m b", r=PACK, b=2),
+                in_=w0_raw[a][:, 2 * G * h : 2 * G * (h + 1)].rearrange("p (m r b) -> p r m b", r=PACK, b=2),
+            )
+
+        def deal_w1(a, h):
+            nc.vector.tensor_copy(
+                out=w1_codes[a, h][:].bitcast(I32).rearrange("p (r m) -> p m r", r=PACK),
+                in_=w1_raw[a, h].bitcast(I32).rearrange("p (m r) -> p m r", r=PACK),
+            )
+
+        def deal_scales(dst, src):
+            nc.vector.tensor_copy(
+                out=dst.rearrange("p (g r m) -> p g r m", r=PACK, m=P),
+                in_=src.rearrange("p (g m r) -> p g r m", r=PACK, m=P),
+            )
+
+        def passes(tap, a, h):
+            for r in range(PACK):
+                cols = slice(P * r, P * (r + 1))
+                if tap == 0:
+                    lhsT = w0_codes[a, h][:, 2 * P * r : 2 * P * (r + 1)].bitcast(FP4X4)
+                    lhsT_scale = s0[a][:, G * h + P * r : G * h + P * (r + 1)]
+                elif tap == 1:
+                    lhsT = w1_codes[a, h][:, cols].bitcast(FP8X4)
+                    lhsT_scale = s1[a][W1_ROW:P, G * h + P * r : G * h + P * (r + 1)]
+                else:
+                    lhsT = w2_codes[a, h][:, cols].bitcast(FP8X4)
+                    lhsT_scale = w2_scales[a, h][:, cols]
+                win = slice(D * tap, D * tap + T)
+                nc.tensor.matmul_mx(
+                    out=acc[h, r][:],
+                    lhsT=lhsT,
+                    lhsT_scale=lhsT_scale,
+                    rhs=x_codes[a][:, win].bitcast(FP8X4),
+                    rhs_scale=x_scales[a][:, win],
+                    start=(tap == 0 and a == 0),
+                    stop=(tap == 2 and a == 1),
+                )
+
+        def drain(engine, h, r):
+            copy(engine, y[h][:, T * r : T * (r + 1)], acc[h, r][:])
+
+        def store_y(h, r0, r1):
+            dst = out_0[G * h : G * (h + 1), :].rearrange("(p r) t -> p (r t)", r=PACK)
+            nc.sync.dma_start(out=dst[:, T * r0 : T * r1], in_=y[h][:, T * r0 : T * r1])
+
+        def store_codes(h, c0, c1):
+            dst = out_1[h].rearrange("p t i -> p (t i)").bitcast(I32)
+            nc.sync.dma_start(out=dst[:, c0:c1], in_=y_codes[h][:, c0:c1].bitcast(I32))
+
+        def store_scales(q, queue):
+            queue.dma_start(
+                out=out_2.rearrange("a (q r) t -> q r a t", r=4)[q].bitcast(I32),
+                in_=y_scales[32 * q : 32 * q + 4, :].bitcast(I32).rearrange("r (a w) -> r a w", a=2),
+            )
+
+        def round_x(engine, a, first, c0, c1):
+            interleave(engine, x_bf[a], x_raw[a, first], c0, c1, first)
+
+        def quantize_x(a, c0, c1):
+            quantize(x_codes[a], x_scales[a], x_bf[a], c0, c1)
+
+        nc.vector.memset(s0_raw[:].bitcast(I32), 0)
+        nc.gpsimd.memset(s1_raw[:].bitcast(I32), 0)
+        load_x(0, 0, 256)
+        load_scales(s0_raw, w0_scales, 0)
+        load_w0(0)
+        load_x(0, 256, 512)
+        load_x(0, 512, XW)
+        load_scales(s1_raw, w1_scales, W1_ROW)
+        load_w1(0, 1, 0, 1)
+        load_x(1, 0, 256)
+        load_x(1, 256, XW)
+        load_w0(1)
+        load_w1(1, 2, 0, 1)
+        load_w2(0, 0, 0, P)
+        load_w2(1, 0, 0, P)
+        load_w1(0, 2, 1, 2)
+        load_w2(0, 1, 0, P)
+        load_w2(1, 1, 0, 64)
+        load_w2(1, 1, 64, P)
+
+        round_x("S", 0, 0, 0, 256)
+        deal_scales(s0[0][:], s0_raw[:, 0:M])
+        deal_w0(0, 0)
+        quantize_x(0, 0, 256)
+        round_x("V", 0, 256, 256, 416)
+        round_x("S", 0, 256, 416, 512)
+        round_x("S", 0, 512, 512, XW)
+        quantize_x(0, 256, 512)
+        passes(0, 0, 0)
+        deal_w0(0, 1)
+        passes(0, 0, 1)
+        quantize_x(0, 512, XW)
+        deal_scales(s1[0][:], s1_raw[:, 0:M])
+        deal_w1(0, 0)
+        passes(1, 0, 0)
+        deal_scales(s0[1][:], s0_raw[:, M : 2 * M])
+        round_x("S", 1, 0, 0, 256)
+        quantize_x(1, 0, 256)
+        round_x("V", 1, 256, 256, 512)
+        round_x("S", 1, 256, 512, XW)
+        deal_w0(1, 0)
+        quantize_x(1, 256, 512)
+        passes(0, 1, 0)
+        deal_scales(s1[1][:], s1_raw[:, M : 2 * M])
+        quantize_x(1, 512, XW)
+        deal_w1(1, 0)
+        passes(1, 1, 0)
+        deal_w0(1, 1)
+        passes(0, 1, 1)
+        round_w2("S", 0, 0, 0, 0, 64)
+        round_w2("V", 0, 0, 0, 64, P)
+        quantize_w2(0, 0, 0, G)
+        passes(2, 0, 0)
+        round_w2("S", 1, 0, 0, 0, 48)
+        round_w2("V", 1, 0, 0, 48, P)
+        for r in range(PACK):
+            quantize_w2(1, 0, P * r, P * (r + 1))
+        passes(2, 1, 0)
+        deal_w1(0, 1)
+        passes(1, 0, 1)
+        deal_w1(1, 1)
+        passes(1, 1, 1)
+        drain("S", 0, 0)
+        drain("S", 0, 1)
+        drain("V", 0, 3)
+        drain("S", 0, 2)
+        store_y(0, 0, 4)
+        round_w2("V", 0, 1, 0, 40, P)
+        round_w2("S", 0, 1, 0, 0, 40)
+        quantize_w2(0, 1, 0, G)
+        passes(2, 0, 1)
+        interleave("S", y_bf[0], y[0], 0, 192)
+        round_w2("V", 1, 1, 0, 0, 64)
+        round_w2("V", 1, 1, 64, 88, P)
+        round_w2("S", 1, 1, 64, 64, 88)
+        for r in range(PACK):
+            quantize_w2(1, 1, P * r, P * (r + 1))
+        passes(2, 1, 1)
+        interleave("S", y_bf[0], y[0], 192, T)
+        quantize(y_codes[0], y_scales, y_bf[0], 0, T)
+        store_codes(0, 0, T)
+        drain("S", 1, 0)
+        drain("V", 1, 1)
+        store_y(1, 0, 2)
+        drain("S", 1, 2)
+        drain("V", 1, 3)
+        store_y(1, 2, 4)
+        interleave("V", y_bf[1], y[1], 0, 256)
+        interleave("S", y_bf[1], y[1], 352, T)
+        interleave("V", y_bf[1], y[1], 256, 352)
+        quantize(y_codes[1], y_scales, y_bf[1], 0, 256, T)
+        quantize(y_codes[1], y_scales, y_bf[1], 256, T, T)
+        store_codes(1, 0, T)
+        for q in range(4):
+            store_scales(q, nc.scalar if q % 2 == 0 else nc.sync)

@@ -37,7 +37,7 @@ def tile_mix_dconv_fm_pl_none_kernel(
         x_bf = [tile("x_bf%d" % a, PACK * XW, BF16) for a in range(2)]
         x_codes = [tile("x_codes%d" % a, XW, U32) for a in range(2)]
         x_scales = [tile("x_scales%d" % a, XW, U8) for a in range(2)]
-        w0_raw = [tile("w0_raw%d" % a, 2 * M, U8) for a in range(2)]
+        w0_raw = {}
         w0_codes = {ah: tile("w0_codes%d%d" % ah, 2 * G, U8) for ah in AH}
         w1_raw = {}
         w1_codes = {ah: tile("w1_codes%d%d" % ah, G, U32) for ah in AH}
@@ -69,8 +69,14 @@ def tile_mix_dconv_fm_pl_none_kernel(
                 in_=x[a * G : (a + 1) * G, c0:c1].rearrange("(p j) t -> p j t", j=PACK),
             )
 
-        def load_w0(a):
-            nc.sync.dma_start(out=w0_raw[a][:].bitcast(I32), in_=w0_words[a].bitcast(I32))
+        def load_w0(a0, a1):
+            raw = tile("w0_raw%d" % a0, 2 * M * (a1 - a0), U8)
+            for a in range(a0, a1):
+                w0_raw[a] = raw[:, 2 * M * (a - a0) : 2 * M * (a - a0 + 1)]
+            nc.sync.dma_start(
+                out=raw[:].bitcast(I32).rearrange("p (a n) -> p a n", a=a1 - a0),
+                in_=w0_words.rearrange("a p n -> p a n")[:, a0:a1].bitcast(I32),
+            )
 
         def load_w1(a0, a1, h0, h1):
             width = G * (h1 - h0)
@@ -185,22 +191,27 @@ def tile_mix_dconv_fm_pl_none_kernel(
         def quantize_x(a, c0, c1):
             quantize(x_codes[a], x_scales[a], x_bf[a], c0, c1)
 
+        def round_y(engine, h, c0, c1):
+            interleave(engine, y_bf[h], y[h], c0, c1)
+
+        def quantize_y(h, c0, c1):
+            quantize(y_codes[h], y_scales, y_bf[h], c0, c1, T * h)
+
         nc.vector.memset(s0_raw[:].bitcast(I32), 0)
         nc.gpsimd.memset(s1_raw[:].bitcast(I32), 0)
         load_x(0, 0, 256)
         load_scales(s0_raw, w0_scales, 0)
-        load_w0(0)
-        load_x(0, 256, 512)
-        load_x(0, 512, XW)
+        load_w0(0, 1)
+        load_x(0, 256, XW)
+        load_w1(0, 1, 0, 2)
         load_scales(s1_raw, w1_scales, W1_ROW)
-        load_w1(0, 1, 0, 1)
-        load_x(1, 0, 256)
-        load_x(1, 256, XW)
-        load_w0(1)
+        load_x(1, 0, XW)
+        load_w0(1, 2)
         load_w1(1, 2, 0, 1)
         load_w2(0, 0, 0, P)
-        load_w2(1, 0, 0, P)
-        load_w1(0, 2, 1, 2)
+        load_w2(1, 0, 0, 64)
+        load_w2(1, 0, 64, P)
+        load_w1(1, 2, 1, 2)
         load_w2(0, 1, 0, P)
         load_w2(1, 1, 0, 64)
         load_w2(1, 1, 64, P)
@@ -209,74 +220,75 @@ def tile_mix_dconv_fm_pl_none_kernel(
         deal_scales(s0[0][:], s0_raw[:, 0:M])
         deal_w0(0, 0)
         quantize_x(0, 0, 256)
-        round_x("V", 0, 256, 256, 416)
-        round_x("S", 0, 256, 416, 512)
-        round_x("S", 0, 512, 512, XW)
+        deal_w0(0, 1)
+        round_x("V", 0, 256, 256, 432)
+        round_x("S", 0, 256, 432, 512)
+        round_x("S", 0, 256, 512, XW)
         quantize_x(0, 256, 512)
         passes(0, 0, 0)
-        deal_w0(0, 1)
         passes(0, 0, 1)
         quantize_x(0, 512, XW)
-        deal_scales(s1[0][:], s1_raw[:, 0:M])
         deal_w1(0, 0)
+        deal_scales(s1[0][:], s1_raw[:, 0:M])
         passes(1, 0, 0)
+        deal_w1(0, 1)
+        passes(1, 0, 1)
         deal_scales(s0[1][:], s0_raw[:, M : 2 * M])
-        round_x("S", 1, 0, 0, 256)
-        quantize_x(1, 0, 256)
-        round_x("V", 1, 256, 256, 512)
-        round_x("S", 1, 256, 512, XW)
-        deal_w0(1, 0)
-        quantize_x(1, 256, 512)
-        passes(0, 1, 0)
         deal_scales(s1[1][:], s1_raw[:, M : 2 * M])
-        quantize_x(1, 512, XW)
+        round_x("V", 1, 0, 0, 320)
+        round_x("S", 1, 0, 320, 512)
+        round_x("S", 1, 0, 512, XW)
+        deal_w0(1, 0)
+        quantize_x(1, 0, 512)
+        passes(0, 1, 0)
         deal_w1(1, 0)
+        quantize_x(1, 512, XW)
         passes(1, 1, 0)
         deal_w0(1, 1)
         passes(0, 1, 1)
-        round_w2("S", 0, 0, 0, 0, 64)
-        round_w2("V", 0, 0, 0, 64, P)
+        round_w2("S", 0, 0, 0, 0, 44)
+        round_w2("V", 0, 0, 0, 44, P)
         quantize_w2(0, 0, 0, G)
         passes(2, 0, 0)
-        round_w2("S", 1, 0, 0, 0, 48)
-        round_w2("V", 1, 0, 0, 48, P)
+        round_w2("S", 1, 0, 0, 0, 44)
+        round_w2("V", 1, 0, 0, 44, 64)
+        round_w2("V", 1, 0, 64, 84, P)
+        round_w2("S", 1, 0, 64, 64, 84)
         for r in range(PACK):
             quantize_w2(1, 0, P * r, P * (r + 1))
         passes(2, 1, 0)
-        deal_w1(0, 1)
-        passes(1, 0, 1)
         deal_w1(1, 1)
         passes(1, 1, 1)
         drain("S", 0, 0)
-        drain("S", 0, 1)
-        drain("V", 0, 3)
+        drain("V", 0, 1)
         drain("S", 0, 2)
+        drain("S", 0, 3)
         store_y(0, 0, 4)
-        round_w2("V", 0, 1, 0, 40, P)
-        round_w2("S", 0, 1, 0, 0, 40)
+        round_w2("V", 0, 1, 0, 24, P)
+        round_w2("S", 0, 1, 0, 0, 24)
+        round_y("S", 0, 0, 320)
         quantize_w2(0, 1, 0, G)
         passes(2, 0, 1)
-        interleave("S", y_bf[0], y[0], 0, 192)
         round_w2("V", 1, 1, 0, 0, 64)
-        round_w2("V", 1, 1, 64, 88, P)
-        round_w2("S", 1, 1, 64, 64, 88)
+        round_w2("S", 1, 1, 64, 64, 84)
+        round_w2("V", 1, 1, 64, 84, P)
+        round_y("S", 0, 320, 512)
         for r in range(PACK):
             quantize_w2(1, 1, P * r, P * (r + 1))
         passes(2, 1, 1)
-        interleave("S", y_bf[0], y[0], 192, T)
-        quantize(y_codes[0], y_scales, y_bf[0], 0, T)
-        store_codes(0, 0, T)
         drain("S", 1, 0)
+        quantize_y(0, 0, T)
+        store_codes(0, 0, T)
         drain("V", 1, 1)
         store_y(1, 0, 2)
         drain("S", 1, 2)
         drain("V", 1, 3)
         store_y(1, 2, 4)
-        interleave("V", y_bf[1], y[1], 0, 256)
-        interleave("S", y_bf[1], y[1], 352, T)
-        interleave("V", y_bf[1], y[1], 256, 352)
-        quantize(y_codes[1], y_scales, y_bf[1], 0, 256, T)
-        quantize(y_codes[1], y_scales, y_bf[1], 256, T, T)
+        round_y("V", 1, 0, 256)
+        round_y("S", 1, 352, T)
+        round_y("V", 1, 256, 352)
+        quantize_y(1, 0, 256)
+        quantize_y(1, 256, T)
         store_codes(1, 0, T)
         for q in range(4):
             store_scales(q, nc.scalar if q % 2 == 0 else nc.sync)

@@ -41,10 +41,8 @@ def tile_mix_dconv_fm_pl_none_kernel(
         w0_codes = {ah: tile("w0_codes%d%d" % ah, 2 * G, U8) for ah in AH}
         w1_raw = {}
         w1_codes = {ah: tile("w1_codes%d%d" % ah, G, U32) for ah in AH}
-        s0_raw = tile("s0_raw", 2 * M, U8)
-        s1_raw = tile("s1_raw", 2 * M, U8)
-        s0 = [tile("s0_%d" % a, M, U8) for a in range(2)]
-        s1 = [tile("s1_%d" % a, M, U8) for a in range(2)]
+        s_raw = tile("s_raw", 2 * M, U8)
+        w_scales = {ah: tile("w_scales%d%d" % ah, G, U8) for ah in AH}
         w2_bf = {ah: tile("w2_bf%d%d" % ah, PACK * G, BF16) for ah in AH}
         w2_codes = {ah: tile("w2_codes%d%d" % ah, G, U32) for ah in AH}
         w2_scales = {ah: tile("w2_scales%d%d" % ah, G, U8) for ah in AH}
@@ -139,10 +137,11 @@ def tile_mix_dconv_fm_pl_none_kernel(
                 in_=w1_raw[a, h].bitcast(I32).rearrange("p (m r) -> p m r", r=PACK),
             )
 
-        def deal_scales(dst, src):
+        def deal_scales(a, h):
+            c0 = M * a + G * h
             nc.vector.tensor_copy(
-                out=dst.rearrange("p (g r m) -> p g r m", r=PACK, m=P),
-                in_=src.rearrange("p (g m r) -> p g r m", r=PACK, m=P),
+                out=w_scales[a, h][:].rearrange("p (r m) -> p r m", r=PACK),
+                in_=s_raw[:, c0 : c0 + G].rearrange("p (m r) -> p r m", r=PACK),
             )
 
         def passes(tap, a, h):
@@ -150,10 +149,10 @@ def tile_mix_dconv_fm_pl_none_kernel(
                 cols = slice(P * r, P * (r + 1))
                 if tap == 0:
                     lhsT = w0_codes[a, h][:, 2 * P * r : 2 * P * (r + 1)].bitcast(FP4X4)
-                    lhsT_scale = s0[a][:, G * h + P * r : G * h + P * (r + 1)]
+                    lhsT_scale = w_scales[a, h][:, cols]
                 elif tap == 1:
                     lhsT = w1_codes[a, h][:, cols].bitcast(FP8X4)
-                    lhsT_scale = s1[a][W1_ROW:P, G * h + P * r : G * h + P * (r + 1)]
+                    lhsT_scale = w_scales[a, h][W1_ROW:P, cols]
                 else:
                     lhsT = w2_codes[a, h][:, cols].bitcast(FP8X4)
                     lhsT_scale = w2_scales[a, h][:, cols]
@@ -197,46 +196,43 @@ def tile_mix_dconv_fm_pl_none_kernel(
         def quantize_y(h, c0, c1):
             quantize(y_codes[h], y_scales, y_bf[h], c0, c1, T * h)
 
-        nc.vector.memset(s0_raw[:].bitcast(I32), 0)
-        nc.gpsimd.memset(s1_raw[:].bitcast(I32), 0)
+        nc.vector.memset(s_raw[:].bitcast(I32), 0)
         load_x(0, 0, 256)
-        load_scales(s0_raw, w0_scales, 0)
+        load_scales(s_raw, w0_scales, 0)
         load_w0(0, 1)
         load_x(0, 256, XW)
-        load_w1(0, 1, 0, 2)
-        load_scales(s1_raw, w1_scales, W1_ROW)
+        load_scales(s_raw, w1_scales, W1_ROW)
+        load_w1(0, 1, 0, 1)
         load_x(1, 0, XW)
         load_w0(1, 2)
         load_w1(1, 2, 0, 1)
         load_w2(0, 0, 0, P)
         load_w2(1, 0, 0, 64)
         load_w2(1, 0, 64, P)
-        load_w1(1, 2, 1, 2)
+        load_w1(0, 2, 1, 2)
         load_w2(0, 1, 0, P)
         load_w2(1, 1, 0, 64)
         load_w2(1, 1, 64, P)
 
         round_x("S", 0, 0, 0, 256)
-        deal_scales(s0[0][:], s0_raw[:, 0:M])
         deal_w0(0, 0)
-        quantize_x(0, 0, 256)
         deal_w0(0, 1)
-        round_x("V", 0, 256, 256, 432)
-        round_x("S", 0, 256, 432, 512)
+        quantize_x(0, 0, 256)
+        round_x("V", 0, 256, 256, 400)
+        round_x("S", 0, 256, 400, 512)
         round_x("S", 0, 256, 512, XW)
+        deal_scales(0, 0)
         quantize_x(0, 256, 512)
         passes(0, 0, 0)
+        deal_scales(0, 1)
         passes(0, 0, 1)
-        quantize_x(0, 512, XW)
         deal_w1(0, 0)
-        deal_scales(s1[0][:], s1_raw[:, 0:M])
+        quantize_x(0, 512, XW)
         passes(1, 0, 0)
-        deal_w1(0, 1)
-        passes(1, 0, 1)
-        deal_scales(s0[1][:], s0_raw[:, M : 2 * M])
-        deal_scales(s1[1][:], s1_raw[:, M : 2 * M])
-        round_x("V", 1, 0, 0, 320)
-        round_x("S", 1, 0, 320, 512)
+        deal_scales(1, 0)
+        deal_scales(1, 1)
+        round_x("V", 1, 0, 0, 256)
+        round_x("S", 1, 0, 256, 512)
         round_x("S", 1, 0, 512, XW)
         deal_w0(1, 0)
         quantize_x(1, 0, 512)
@@ -246,8 +242,8 @@ def tile_mix_dconv_fm_pl_none_kernel(
         passes(1, 1, 0)
         deal_w0(1, 1)
         passes(0, 1, 1)
-        round_w2("S", 0, 0, 0, 0, 44)
-        round_w2("V", 0, 0, 0, 44, P)
+        round_w2("S", 0, 0, 0, 0, 56)
+        round_w2("V", 0, 0, 0, 56, P)
         quantize_w2(0, 0, 0, G)
         passes(2, 0, 0)
         round_w2("S", 1, 0, 0, 0, 44)
@@ -257,22 +253,25 @@ def tile_mix_dconv_fm_pl_none_kernel(
         for r in range(PACK):
             quantize_w2(1, 0, P * r, P * (r + 1))
         passes(2, 1, 0)
-        deal_w1(1, 1)
-        passes(1, 1, 1)
+        deal_w1(0, 1)
+        passes(1, 0, 1)
         drain("S", 0, 0)
         drain("V", 0, 1)
+        deal_w1(1, 1)
+        passes(1, 1, 1)
         drain("S", 0, 2)
         drain("S", 0, 3)
         store_y(0, 0, 4)
-        round_w2("V", 0, 1, 0, 24, P)
-        round_w2("S", 0, 1, 0, 0, 24)
+        round_w2("V", 0, 1, 0, 32, P)
+        round_w2("S", 0, 1, 0, 0, 32)
         round_y("S", 0, 0, 320)
-        quantize_w2(0, 1, 0, G)
+        for r in range(PACK):
+            quantize_w2(0, 1, P * r, P * (r + 1))
         passes(2, 0, 1)
         round_w2("V", 1, 1, 0, 0, 64)
         round_w2("S", 1, 1, 64, 64, 84)
         round_w2("V", 1, 1, 64, 84, P)
-        round_y("S", 0, 320, 512)
+        round_y("S", 0, 320, T)
         for r in range(PACK):
             quantize_w2(1, 1, P * r, P * (r + 1))
         passes(2, 1, 1)

from contextlib import ExitStack

import concourse.mybir as mybir

D, K, M, T = 64, 1024, 1024, 512
FLOPS = 2 * 3 * K * M * T

F32 = mybir.dt.float32
BF16 = mybir.dt.bfloat16
I32 = mybir.dt.int32
U32 = mybir.dt.uint32
U8 = mybir.dt.uint8
FP8X4 = mybir.dt.float8_e4m3fn_x4
FP4X4 = mybir.dt.float4_e2m1fn_x4

P = 128
PACK = 4
G = P * PACK
XW = T + 2 * D
W1_ROW = 4


def tile_mix_dconv_fm_pl_none_kernel(
    tc, x, w0_words, w0_scales, w1_words, w1_scales, w2, out_0, out_1, out_2
):
    nc = tc.nc
    with ExitStack() as ctx:
        sb = ctx.enter_context(tc.tile_pool(name="sb", bufs=1))
        ps = ctx.enter_context(tc.psum_pool(name="ps", bufs=1))
        ctx.enter_context(tc.manual_schedule())

        def tile(name, width, dtype):
            return sb.tile([P, width], dtype, name=name, align_bytes=64)

        AH = [(a, h) for a in range(2) for h in range(2)]
        x_raw = {}
        x_bf = [tile("x_bf%d" % a, PACK * XW, BF16) for a in range(2)]
        x_codes = [tile("x_codes%d" % a, XW, U32) for a in range(2)]
        x_scales = [tile("x_scales%d" % a, XW, U8) for a in range(2)]
        w0_raw = {}
        w0_codes = {ah: tile("w0_codes%d%d" % ah, 2 * G, U8) for ah in AH}
        w1_raw = {}
        w1_codes = {ah: tile("w1_codes%d%d" % ah, G, U32) for ah in AH}
        s_raw = tile("s_raw", 2 * M, U8)
        w_scales = {ah: tile("w_scales%d%d" % ah, G, U8) for ah in AH}
        w2_bf = {ah: tile("w2_bf%d%d" % ah, PACK * G, BF16) for ah in AH}
        w2_codes = {ah: tile("w2_codes%d%d" % ah, G, U32) for ah in AH}
        w2_scales = {ah: tile("w2_scales%d%d" % ah, G, U8) for ah in AH}
        y = [tile("y%d" % h, PACK * T, F32) for h in range(2)]
        y_bf = [tile("y_bf%d" % h, PACK * T, BF16) for h in range(2)]
        y_codes = [tile("y_codes%d" % h, T, U32) for h in range(2)]
        y_scales = tile("y_scales", 2 * T, U8)
        acc = {(h, r): ps.tile([P, T], F32, name="acc%d%d" % (h, r)) for h in range(2) for r in range(PACK)}
        w2_raw = {}

        def copy(engine, out, in_):
            if engine == "V":
                nc.vector.tensor_copy(out=out, in_=in_)
            else:
                nc.scalar.copy(out=out, in_=in_)

        def load_x(a, c0, c1):
            raw = tile("x_raw%d_%d" % (a, c0), PACK * (c1 - c0), F32)
            x_raw[a, c0] = raw
            nc.sync.dma_start(
                out=raw[:].rearrange("p (j t) -> p j t", j=PACK),
                in_=x[a * G : (a + 1) * G, c0:c1].rearrange("(p j) t -> p j t", j=PACK),
            )

        def load_w0(a0, a1):
            raw = tile("w0_raw%d" % a0, 2 * M * (a1 - a0), U8)
            for a in range(a0, a1):
                w0_raw[a] = raw[:, 2 * M * (a - a0) : 2 * M * (a - a0 + 1)]
            nc.sync.dma_start(
                out=raw[:].bitcast(I32).rearrange("p (a n) -> p a n", a=a1 - a0),
                in_=w0_words.rearrange("a p n -> p a n")[:, a0:a1].bitcast(I32),
            )

        def load_w1(a0, a1, h0, h1):
            width = G * (h1 - h0)
            raw = tile("w1_raw%d%d" % (a0, h0), width * (a1 - a0), U32)
            for a in range(a0, a1):
                for h in range(h0, h1):
                    c0 = width * (a - a0) + G * (h - h0)
                    w1_raw[a, h] = raw[:, c0 : c0 + G]
            src = w1_words.rearrange("a p n i -> p a (n i)")[:, a0:a1, PACK * G * h0 : PACK * G * h1]
            nc.sync.dma_start(
                out=raw[:].bitcast(I32).rearrange("p (a n) -> p a n", a=a1 - a0), in_=src.bitcast(I32)
            )

        def load_scales(raw, src, row):
            for r in range(4):
                nc.sync.dma_start(
                    out=raw[row + r : P : 32, :].bitcast(I32).rearrange("q (a w) -> q a w", a=2),
                    in_=src.rearrange("a (q r) n -> r q a n", r=4)[r].bitcast(I32),
                )

        def load_w2(a, h, m0, m1):
            width = PACK * (m1 - m0)
            raw = tile("w2_raw%d%d_%d" % (a, h, m0), PACK * width, F32)
            w2_raw[a, h, m0] = raw
            n0 = G * h + PACK * m0
            nc.sync.dma_start(
                out=raw[:].rearrange("p (j n) -> p j n", j=PACK),
                in_=w2[a * G : (a + 1) * G, n0 : n0 + width].rearrange("(p j) n -> p j n", j=PACK),
            )

        def interleave(engine, dst, src, c0, c1, first=0):
            out = dst[:, PACK * c0 : PACK * c1].rearrange("p (c i j) -> p c j i", i=4, j=PACK)
            in_ = src[:].rearrange("p (j t) -> p j t", j=PACK)[:, :, c0 - first : c1 - first].rearrange("p j (c i) -> p c j i", i=4)
            copy(engine, out, in_)

        def quantize(codes, scales, src, c0, c1, s_off=0):
            nc.vector.quantize_mx(
                out=codes[:, c0:c1].bitcast(FP8X4),
                scales=scales[:, s_off + c0 : s_off + c1],
                in_=src[:, PACK * c0 : PACK * c1],
            )

        def round_w2(engine, a, h, piece, m0, m1):
            out = w2_bf[a, h][:].rearrange("p (r m j) -> p m j r", r=PACK, j=PACK)[:, m0:m1]
            in_ = w2_raw[a, h, piece][:].rearrange("p (j m r) -> p m j r", r=PACK, j=PACK)[:, m0 - piece : m1 - piece]
            copy(engine, out, in_)

        def quantize_w2(a, h, c0, c1):
            quantize(w2_codes[a, h], w2_scales[a, h], w2_bf[a, h], c0, c1)

        def deal_w0(a, h):
            nc.vector.tensor_copy(
                out=w0_codes[a, h][:].rearrange("p (r m b) -> p r m b", r=PACK, b=2),
                in_=w0_raw[a][:, 2 * G * h : 2 * G * (h + 1)].rearrange("p (m r b) -> p r m b", r=PACK, b=2),
            )

        def deal_w1(a, h):
            nc.vector.tensor_copy(
                out=w1_codes[a, h][:].bitcast(I32).rearrange("p (r m) -> p m r", r=PACK),
                in_=w1_raw[a, h].bitcast(I32).rearrange("p (m r) -> p m r", r=PACK),
            )

        def deal_scales(a, h):
            c0 = M * a + G * h
            nc.vector.tensor_copy(
                out=w_scales[a, h][:].rearrange("p (r m) -> p r m", r=PACK),
                in_=s_raw[:, c0 : c0 + G].rearrange("p (m r) -> p r m", r=PACK),
            )

        def passes(tap, a, h):
            for r in range(PACK):
                cols = slice(P * r, P * (r + 1))
                if tap == 0:
                    lhsT = w0_codes[a, h][:, 2 * P * r : 2 * P * (r + 1)].bitcast(FP4X4)
                    lhsT_scale = w_scales[a, h][:, cols]
                elif tap == 1:
                    lhsT = w1_codes[a, h][:, cols].bitcast(FP8X4)
                    lhsT_scale = w_scales[a, h][W1_ROW:P, cols]
                else:
                    lhsT = w2_codes[a, h][:, cols].bitcast(FP8X4)
                    lhsT_scale = w2_scales[a, h][:, cols]
                win = slice(D * tap, D * tap + T)
                nc.tensor.matmul_mx(
                    out=acc[h, r][:],
                    lhsT=lhsT,
                    lhsT_scale=lhsT_scale,
                    rhs=x_codes[a][:, win].bitcast(FP8X4),
                    rhs_scale=x_scales[a][:, win],
                    start=(tap == 0 and a == 0),
                    stop=(tap == 2 and a == 1),
                )

        def drain(engine, h, r):
            copy(engine, y[h][:, T * r : T * (r + 1)], acc[h, r][:])

        def store_y(h, r0, r1):
            dst = out_0[G * h : G * (h + 1), :].rearrange("(p r) t -> p (r t)", r=PACK)
            nc.sync.dma_start(out=dst[:, T * r0 : T * r1], in_=y[h][:, T * r0 : T * r1])

        def store_codes(h, c0, c1):
            dst = out_1[h].rearrange("p t i -> p (t i)").bitcast(I32)
            nc.sync.dma_start(out=dst[:, c0:c1], in_=y_codes[h][:, c0:c1].bitcast(I32))

        def store_scales(q, queue):
            queue.dma_start(
                out=out_2.rearrange("a (q r) t -> q r a t", r=4)[q].bitcast(I32),
                in_=y_scales[32 * q : 32 * q + 4, :].bitcast(I32).rearrange("r (a w) -> r a w", a=2),
            )

        def round_x(engine, a, first, c0, c1):
            interleave(engine, x_bf[a], x_raw[a, first], c0, c1, first)

        def quantize_x(a, c0, c1):
            quantize(x_codes[a], x_scales[a], x_bf[a], c0, c1)

        def round_y(engine, h, c0, c1):
            interleave(engine, y_bf[h], y[h], c0, c1)

        def quantize_y(h, c0, c1):
            quantize(y_codes[h], y_scales, y_bf[h], c0, c1, T * h)

        nc.vector.memset(s_raw[:].bitcast(I32), 0)
        load_x(0, 0, 256)
        load_scales(s_raw, w0_scales, 0)
        load_w0(0, 1)
        load_x(0, 256, XW)
        load_scales(s_raw, w1_scales, W1_ROW)
        load_w1(0, 1, 0, 1)
        load_x(1, 0, XW)
        load_w0(1, 2)
        load_w1(1, 2, 0, 1)
        load_w2(0, 0, 0, P)
        load_w2(1, 0, 0, 64)
        load_w2(1, 0, 64, P)
        load_w1(0, 2, 1, 2)
        load_w2(0, 1, 0, P)
        load_w2(1, 1, 0, 64)
        load_w2(1, 1, 64, P)

        round_x("S", 0, 0, 0, 256)
        deal_w0(0, 0)
        deal_w0(0, 1)
        quantize_x(0, 0, 256)
        round_x("V", 0, 256, 256, 400)
        round_x("S", 0, 256, 400, 512)
        round_x("S", 0, 256, 512, XW)
        deal_scales(0, 0)
        quantize_x(0, 256, 512)
        passes(0, 0, 0)
        deal_scales(0, 1)
        passes(0, 0, 1)
        deal_w1(0, 0)
        quantize_x(0, 512, XW)
        passes(1, 0, 0)
        deal_scales(1, 0)
        deal_scales(1, 1)
        round_x("V", 1, 0, 0, 256)
        round_x("S", 1, 0, 256, 512)
        round_x("S", 1, 0, 512, XW)
        deal_w0(1, 0)
        quantize_x(1, 0, 512)
        passes(0, 1, 0)
        deal_w1(1, 0)
        quantize_x(1, 512, XW)
        passes(1, 1, 0)
        deal_w0(1, 1)
        passes(0, 1, 1)
        round_w2("S", 0, 0, 0, 0, 56)
        round_w2("V", 0, 0, 0, 56, P)
        quantize_w2(0, 0, 0, G)
        passes(2, 0, 0)
        round_w2("S", 1, 0, 0, 0, 44)
        round_w2("V", 1, 0, 0, 44, 64)
        round_w2("V", 1, 0, 64, 84, P)
        round_w2("S", 1, 0, 64, 64, 84)
        for r in range(PACK):
            quantize_w2(1, 0, P * r, P * (r + 1))
        passes(2, 1, 0)
        deal_w1(0, 1)
        passes(1, 0, 1)
        drain("S", 0, 0)
        drain("V", 0, 1)
        deal_w1(1, 1)
        passes(1, 1, 1)
        drain("S", 0, 2)
        drain("S", 0, 3)
        store_y(0, 0, 4)
        round_w2("V", 0, 1, 0, 32, P)
        round_w2("S", 0, 1, 0, 0, 32)
        round_y("S", 0, 0, 320)
        for r in range(PACK):
            quantize_w2(0, 1, P * r, P * (r + 1))
        passes(2, 0, 1)
        round_w2("V", 1, 1, 0, 0, 64)
        round_w2("S", 1, 1, 64, 64, 84)
        round_w2("V", 1, 1, 64, 84, P)
        round_y("S", 0, 320, T)
        for r in range(PACK):
            quantize_w2(1, 1, P * r, P * (r + 1))
        passes(2, 1, 1)
        drain("S", 1, 0)
        quantize_y(0, 0, T)
        store_codes(0, 0, T)
        drain("V", 1, 1)
        store_y(1, 0, 2)
        drain("S", 1, 2)
        drain("V", 1, 3)
        store_y(1, 2, 4)
        round_y("V", 1, 0, 256)
        round_y("S", 1, 352, T)
        round_y("V", 1, 256, 352)
        quantize_y(1, 0, 256)
        quantize_y(1, 256, T)
        store_codes(1, 0, T)
        for q in range(4):
            store_scales(q, nc.scalar if q % 2 == 0 else nc.sync)
